import numpy as np
import ml_dtypes


def mxq(x, axis, fmt="e4m3"):
    dtype, down = {"e4m3": (ml_dtypes.float8_e4m3fn, 7), "e5m2": (ml_dtypes.float8_e5m2, 14)}[fmt]
    v = np.moveaxis(np.asarray(x, np.float32).astype(ml_dtypes.bfloat16).astype(np.float64), axis, -1)
    blocks = v.reshape(v.shape[:-1] + (-1, 32))
    amax = np.abs(blocks).max(-1, keepdims=True)
    byte = np.maximum(np.where(amax > 0, np.frexp(amax)[1] - 1 + 127, 0) - down, 1)
    scale = np.exp2(byte - 127.0)
    codes = (blocks / scale).astype(np.float32).astype(dtype).astype(np.float64)
    return np.moveaxis((codes * scale).reshape(v.shape), -1, axis)


WIDE = False


def mx_kscale(k):
    if not WIDE:
        return np.ones(k)
    levels = np.array([10, -10, 5, -5, 0])
    if k % 512:
        return np.exp2(np.random.permutation(np.resize(levels, k // 32))).repeat(32)
    a = np.empty((k // 512, 16))
    for p in range(k // 512):
        a[p, :8] = np.random.permutation(np.resize(levels, 8))
        for g in range(8):
            far = levels[np.abs(levels - a[p, g]) >= 10]
            a[p, g + 8] = far[np.random.randint(len(far))]
    return np.exp2(a.ravel()).repeat(32)


def f64(x):
    return np.asarray(x).astype(np.float64)


def striped(idx):
    return np.tile(np.asarray(idx).reshape(-1, 16).T, (8, 1)).astype(np.uint16)


def unstriped(offs):
    return offs[:16].T.reshape(-1).astype(np.int64)


E2M1 = np.array([0.0, 0.5, 1.0, 1.5, 2.0, 3.0, 4.0, 6.0, -0.0, -0.5, -1.0, -1.5, -2.0, -3.0, -4.0, -6.0])


def pack_weight(w, fmt):
    k, n = w.shape
    w = f64(np.asarray(w, np.float32).astype(ml_dtypes.bfloat16)).reshape(k // 32, 32, n)
    amax = np.abs(w).max(1)
    if fmt == "e4m3":
        byte = np.frexp(amax)[1] - 1 + 127 - 7
    else:
        mant, ex = np.frexp(amax / 6.0)
        byte = np.where(mant > 0.5, ex, ex - 1) + 127
    byte = np.clip(np.where(amax > 0, byte, 1), 1, 254)
    scaled = (w * np.exp2(127.0 - byte)[:, None, :]).reshape(k, n).astype(np.float32)
    by_word = np.ascontiguousarray(scaled.reshape(k // 512, 128, 4, n).transpose(0, 1, 3, 2))
    if fmt == "e4m3":
        words = by_word.astype(ml_dtypes.float8_e4m3fn).view(np.uint8)
    else:
        c = by_word.astype(ml_dtypes.float4_e2m1fn).view(np.uint8) & 0xF
        words = (c[..., 0::2] | (c[..., 1::2] << 4)).reshape(k // 512, 128, 2 * n)
    return np.ascontiguousarray(words), np.ascontiguousarray(byte.astype(np.uint8).reshape(k // 512, 16, n))


def unpack_weight(words, scales, fmt):
    g, _, n = scales.shape
    words = np.ascontiguousarray(words).reshape(g, 128, n, -1)
    if fmt == "e4m3":
        vals = words.view(ml_dtypes.float8_e4m3fn).astype(np.float64)
    else:
        nib = np.empty((g, 128, n, 4), np.uint8)
        nib[..., 0::2] = words & 0xF
        nib[..., 1::2] = words >> 4
        vals = E2M1[nib]
    vals = vals * np.repeat(np.exp2(scales.astype(np.float64) - 127.0), 8, axis=1)[..., None]
    return vals.transpose(0, 1, 3, 2).reshape(g * 512, n)


D, E, T, I, Q = 512, 512, 2048, 512, 128


def setup_inputs():
    n = np.random.standard_normal
    idx = np.random.permutation(T)[:I]
    fd = mx_kscale(D)
    fe = mx_kscale(E)
    keysp = pack_weight(n((D, T)) / fd[:, None], "e4m3")
    valsp = pack_weight(n((E, T)) / fe[:, None], "e4m3")
    return {
        "query": (n((D, Q)) * 0.8 / np.sqrt(D) * fd[:, None]).astype(np.float32),
        "keys_words": keysp[0],
        "keys_scales": keysp[1],
        "averse": (np.random.uniform(0.4, 1.0, (Q, 1))).astype(np.float32),
        "gout": (n((E, Q)) * 1 / np.sqrt(E) * fe[:, None]).astype(np.float32),
        "vals_words": valsp[0],
        "vals_scales": valsp[1],
        "base": (0.5 * n((Q, I))).astype(np.float32),
        "offs": striped(idx),
    }


def reference(query, keys_words, keys_scales, averse, gout, vals_words, vals_scales, base, offs):
    idx = unstriped(offs)
    keysu = unpack_weight(keys_words, keys_scales, "e4m3")
    valsu = unpack_weight(vals_words, vals_scales, "e4m3")
    queryq = mxq(f64(query), 0, "e4m3")
    keysidxg = keysu[:, idx]
    a = queryq.T @ keysidxg
    p = np.exp(a - np.max(a, axis=1, keepdims=True))
    p2 = np.exp(a * (-1.0) - np.max(a * (-1.0), axis=1, keepdims=True))
    goutq = mxq(f64(gout), 0, "e4m3")
    valsidxg = valsu[:, idx]
    c0 = goutq.T @ valsidxg
    dr2 = c0 * (-1.0) * f64(averse)
    dp2 = dr2 / np.sum(p2, axis=1, keepdims=True) + np.sum(dr2 * p2 / np.square(np.sum(p2, axis=1, keepdims=True)) * (-1.0), axis=1, keepdims=True)
    dp = c0 / np.sum(p, axis=1, keepdims=True) + np.sum(c0 * p / np.square(np.sum(p, axis=1, keepdims=True)) * (-1.0), axis=1, keepdims=True)
    da = dp * p - dp2 * p2
    hda = da * 512.0 * 2.0 * 512.0
    hdp = hda * p
    hdp2 = hda * (-1.0) * p2
    hp2 = hda * (-1.0) * dp2 + np.sum(hdp2 * dr2 / np.square(np.sum(p2, axis=1, keepdims=True)) * (-1.0), axis=1, keepdims=True) + np.sum(hdp2, axis=1, keepdims=True) * (-1.0) / np.square(np.sum(p2, axis=1, keepdims=True)) * dr2 + np.sum(np.sum(hdp2, axis=1, keepdims=True) * (-1.0) * dr2 * p2 / np.square(np.square(np.sum(p2, axis=1, keepdims=True))) * (-1.0), axis=1, keepdims=True) * np.sum(p2, axis=1, keepdims=True) * 2.0
    hp = hda * dp + np.sum(hdp * c0 / np.square(np.sum(p, axis=1, keepdims=True)) * (-1.0), axis=1, keepdims=True) + np.sum(hdp, axis=1, keepdims=True) * (-1.0) / np.square(np.sum(p, axis=1, keepdims=True)) * c0 + np.sum(np.sum(hdp, axis=1, keepdims=True) * (-1.0) * c0 * p / np.square(np.square(np.sum(p, axis=1, keepdims=True))) * (-1.0), axis=1, keepdims=True) * np.sum(p, axis=1, keepdims=True) * 2.0
    ha = hp * p - hp2 * p2
    y = ha + f64(base)
    return y

@@ -1,0 +1,222 @@
+import math
+from contextlib import ExitStack
+
+import concourse.mybir as mybir
+
+F32 = mybir.dt.float32
+BF16 = mybir.dt.bfloat16
+I32 = mybir.dt.int32
+U32 = mybir.dt.uint32
+U16 = mybir.dt.uint16
+U8 = mybir.dt.uint8
+FP8X4 = mybir.dt.float8_e4m3fn_x4
+ALU = mybir.AluOpType
+ACT = mybir.ActivationFunctionType
+AX = mybir.AxisListType
+
+P = 128
+PACK = 4
+POOL = 2048
+SLOTS = 512
+ROWS = 128
+FEATS = 512
+HALF = SLOTS // 2
+H = math.sqrt(512.0 * 2.0 * 512.0) / 2.0
+
+FLOPS = 2 * 2 * FEATS * ROWS * SLOTS
+
+
+def tile_attend_gpdirect_twoside_kernel(
+    tc, query, keys_words, keys_scales, averse, gout, vals_words, vals_scales, base, offs, out
+):
+    nc = tc.nc
+    with ExitStack() as ctx:
+        sb = ctx.enter_context(tc.tile_pool(name="sb", bufs=1))
+        psum = ctx.enter_context(tc.psum_pool(name="psum", bufs=1))
+
+        def wide(name):
+            return sb.tile([P, SLOTS], F32, name=name)
+
+        def col(name):
+            return sb.tile([P, 1], F32, name=name)
+
+        def fma(name, x, scale, bias=None):
+            t = col(name)
+            if bias is None:
+                nc.scalar.activation(t[:], x, ACT.Identity, scale=scale)
+            else:
+                nc.scalar.activation(t[:], x, ACT.Identity, bias=bias, scale=scale)
+            return t
+
+        def load_scales(tile, scales):
+            for quad in range(4):
+                nc.sync.dma_start(
+                    out=tile[32 * quad : 32 * quad + 4, :].bitcast(I32),
+                    in_=scales[0, 4 * quad : 4 * quad + 4, :].bitcast(I32),
+                )
+
+        def load_words(tile, words):
+            nc.sync.dma_start(
+                out=tile[:].bitcast(I32),
+                in_=words[0].rearrange("p n t -> p (n t)").bitcast(I32),
+            )
+
+        def load_rows(tile, rows):
+            nc.sync.dma_start(out=tile[:], in_=rows.rearrange("(p j) w -> p j w", j=PACK))
+
+        def interleave(name, raw):
+            grouped = sb.tile([P, ROWS, PACK], BF16, name=name, tag=name, align_bytes=64)
+            nc.scalar.copy(out=grouped[:], in_=raw[:].rearrange("p j w -> p w j"))
+            return grouped
+
+        def quantise(name, grouped):
+            codes = sb.tile([P, ROWS], U32, name=name + "_codes", align_bytes=64)
+            plane = sb.tile([P, ROWS], U8, name=name + "_plane", align_bytes=64)
+            nc.vector.quantize_mx(
+                out=codes[:].bitcast(FP8X4),
+                scales=plane[:],
+                in_=grouped[:].rearrange("p w j -> p (w j)"),
+            )
+            return codes, plane
+
+        halves = [slice(0, HALF), slice(HALF, SLOTS)]
+
+        def gather_plane(name, window, tag):
+            picked = sb.tile([P, SLOTS], U8, name=name, tag=tag, align_bytes=64)
+            nc.vector.tensor_copy(out=picked[:], in_=window[:].indirect(offsets[:]))
+            return picked
+
+        def product(name, left, window, plane, tags):
+            bank = psum.tile([P, SLOTS], F32, name=name)
+            for j, cols in enumerate(halves):
+                words = sb.tile([P, HALF], U32, name=f"{name}_words{j}", tag=tags[j], align_bytes=64)
+                entries = offsets[:, j * HALF // 16 : (j + 1) * HALF // 16]
+                nc.vector.tensor_copy(out=words[:], in_=window[:].indirect(entries))
+                nc.tensor.matmul_mx(
+                    out=bank[:, cols],
+                    lhsT=left[0][:].bitcast(FP8X4),
+                    lhsT_scale=left[1][:],
+                    rhs=words[:].bitcast(FP8X4),
+                    rhs_scale=plane[:, cols],
+                    start=True,
+                    stop=True,
+                )
+            return bank
+
+        offsets = sb.tile([P, SLOTS // 16], U16, name="offsets")
+        ks_pool = sb.tile([P, POOL], U8, name="ks_pool", tag="value_words")
+        vs_pool = sb.tile([P, POOL], U8, name="vs_pool", tag="value_scales")
+        q_raw = sb.tile([P, PACK, ROWS], F32, name="q_raw", tag="staging")
+        v = col("v")
+        one = sb.tile([P, 1], F32, name="one", tag="key_words", align_bytes=64)
+        factors = sb.tile([P, 2], F32, name="factors")
+        hv = factors[:, 1:2]
+
+        nc.vector.memset(one[:], 1.0)
+        nc.vector.memset(ks_pool[:].bitcast(I32), 0)
+        nc.vector.tensor_scalar(factors[:, 0:1], one[:], H, None, ALU.mult)
+        nc.vector.memset(vs_pool[:].bitcast(I32), 0)
+
+        nc.sync.dma_start(offsets[:], offs)
+        nc.sync.dma_start(out=v[:], in_=averse)
+        load_rows(q_raw, query)
+        load_scales(ks_pool, keys_scales)
+        kw_pool = sb.tile([P, POOL], U32, name="kw_pool", tag="key_words", align_bytes=64)
+        load_words(kw_pool, keys_words)
+        load_scales(vs_pool, vals_scales)
+
+        q_bf = interleave("q_bf", q_raw)
+        g_raw = sb.tile([P, PACK, ROWS], F32, name="g_raw", tag="staging")
+        load_rows(g_raw, gout)
+        ks = gather_plane("ks", ks_pool, "key_plane")
+        vw_pool = sb.tile([P, POOL], U32, name="vw_pool", tag="value_words")
+        load_words(vw_pool, vals_words)
+        g_bf = interleave("g_bf", g_raw)
+
+        nc.scalar.activation(hv, v[:], ACT.Identity, scale=H)
+        neg_hv = fma("neg_hv", v[:], -H)
+        neg_v = fma("neg_v", v[:], -1.0)
+
+        q_mx = quantise("q", q_bf)
+        a = product("a", q_mx, kw_pool, ks, ("q_bf", "a1"))
+        vs = gather_plane("vs", vs_pool, "key_words")
+
+        base_sb = sb.tile([P, SLOTS], F32, name="base_sb", tag="key_plane", align_bytes=64)
+        nc.sync.dma_start(out=base_sb[:], in_=base)
+
+        neg_max = sb.tile([P, 1], F32, name="neg_max", tag="value_scales")
+        low = col("low")
+        nc.vector.tensor_reduce(out=neg_max[:], in_=a[:], axis=AX.X, op=ALU.max, negate=True)
+        nc.vector.tensor_reduce(out=low[:], in_=a[:], axis=AX.X, op=ALU.min)
+        g_mx = quantise("g", g_bf)
+        p1 = sb.tile([P, SLOTS], F32, name="p1", tag="staging")
+        p2 = wide("p2")
+        sums = sb.tile([P, 2], F32, name="sums")
+        nc.scalar.activation(p1[:], a[:], ACT.Exp, bias=neg_max[:], scale=1.0, accum_out=sums[:, 0:1])
+        nc.scalar.activation(p2[:], a[:], ACT.Exp, bias=low[:], scale=-1.0, accum_out=sums[:, 1:2])
+        k0 = col("k0")
+        nc.scalar.activation(k0[:], low[:], ACT.Exp, bias=neg_max[:], scale=1.0)
+        c = product("c", g_mx, vw_pool, vs, ("g_bf", "c1"))
+
+        inv = sb.tile([P, 2], F32, name="inv", tag="value_words")
+        nc.vector.reciprocal(out=inv[:], in_=sums[:])
+        i1, i2 = inv[:, 0:1], inv[:, 1:2]
+        hi, k = sb.tile([P, 2], F32, name="hi"), col("k")
+        nc.vector.tensor_tensor(hi[:], inv[:], factors[:], ALU.mult)
+        nc.vector.tensor_scalar(k[:], k0[:], i1, i2, ALU.mult, ALU.mult)
+        r1, r2 = wide("r1"), wide("r2")
+        nc.scalar.activation(r2[:], p2[:], ACT.Identity, scale=i2)
+        sc2 = fma("sc2", k[:], -H)
+        sc1 = fma("sc1", k[:], neg_hv[:])
+        kv = fma("kv", k[:], v[:])
+        nc.scalar.activation(r1[:], p1[:], ACT.Identity, scale=i1)
+
+        x1, m1 = wide("x1"), col("m1")
+        nc.vector.scalar_tensor_tensor(x1[:], c[:], hi[:, 0:1], p1[:], ALU.mult, ALU.mult, accum_out=m1[:])
+        x2, m2 = wide("x2"), col("m2")
+        nc.vector.scalar_tensor_tensor(x2[:], c[:], hi[:, 1:2], p2[:], ALU.mult, ALU.mult, accum_out=m2[:])
+        u1, u2 = wide("u1"), wide("u2")
+        nc.vector.scalar_tensor_tensor(u2[:], r2[:], m2[:], x2[:], ALU.mult, ALU.subtract)
+        nc.vector.scalar_tensor_tensor(u1[:], r1[:], m1[:], x1[:], ALU.mult, ALU.subtract)
+
+        b2 = fma("b2", m1[:], k[:])
+        b1 = fma("b1", m2[:], k[:])
+        scratch = [wide(f"scratch{j}") for j in range(3)]
+        f1, f2, spread = col("f1"), col("f2"), col("spread")
+        nc.scalar.activation(scratch[0][:], c[:], ACT.Identity, bias=b2[:], scale=sc2[:], accum_out=f2[:])
+        dm = fma("dm", m1[:], neg_v[:], m2[:])
+        nc.scalar.activation(scratch[1][:], c[:], ACT.Identity, bias=b1[:], scale=sc1[:], accum_out=f1[:])
+        t = fma("t", f2[:], dm[:])
+        nc.scalar.activation(scratch[2][:], c[:], ACT.Square, bias=m1[:], scale=-H, accum_out=spread[:])
+
+        y = sb.tile([P, 2], F32, name="y")
+        y1, y2 = y[:, 0:1], y[:, 1:2]
+        w1, w2 = wide("w1"), wide("w2")
+        nc.vector.scalar_tensor_tensor(w2[:], u2[:], f2[:], r2[:], ALU.add, ALU.mult, accum_out=y2)
+        nc.vector.scalar_tensor_tensor(w1[:], u1[:], f1[:], r1[:], ALU.add, ALU.mult, accum_out=y1)
+
+        sq1, sq2, total1, total2 = wide("sq1"), wide("sq2"), col("total1"), col("total2")
+        nc.scalar.activation(sq2[:], u2[:], ACT.Square, bias=y2, scale=-2.0, accum_out=total2[:])
+        nc.scalar.activation(sq1[:], u1[:], ACT.Square, bias=y1, scale=-2.0, accum_out=total1[:])
+
+        cross = col("cross")
+        nc.vector.tensor_scalar(cross[:], spread[:], kv[:], t[:], ALU.mult, ALU.add)
+        yy, rest = sb.tile([P, 2], F32, name="yy"), sb.tile([P, 2], F32, name="rest")
+        nc.vector.tensor_tensor(yy[:], y[:], y[:], ALU.mult)
+        nc.vector.tensor_scalar(rest[:], yy[:], -SLOTS / 4.0, cross[:], ALU.mult, ALU.add)
+        kc1 = fma("kc1", rest[:, 0:1], 4.0, total1[:])
+        kc2 = fma("kc2", rest[:, 1:2], 4.0, total2[:])
+
+        ta = [sb.tile([P, HALF], F32, name=f"ta{j}") for j in range(2)]
+        tb = [sb.tile([P, HALF], F32, name=f"tb{j}") for j in range(2)]
+        td = [sb.tile([P, HALF], F32, name=f"td{j}") for j in range(2)]
+        res = [sb.tile([P, HALF], F32, name=f"res{j}") for j in range(2)]
+        for j, cols in enumerate(halves):
+            nc.vector.scalar_tensor_tensor(ta[j][:], sq2[:, cols], yy[:, 1:2], base_sb[:, cols], ALU.subtract, ALU.subtract)
+        for j, cols in enumerate(halves):
+            nc.vector.scalar_tensor_tensor(tb[j][:], sq1[:, cols], yy[:, 0:1], ta[j][:], ALU.subtract, ALU.subtract)
+        for j, cols in enumerate(halves):
+            nc.vector.scalar_tensor_tensor(td[j][:], r1[:, cols], kc1[:], tb[j][:], ALU.mult, ALU.subtract)
+        for j, cols in enumerate(halves):
+            nc.vector.scalar_tensor_tensor(res[j][:], r2[:, cols], kc2[:], td[j][:], ALU.mult, ALU.subtract)
+            nc.sync.dma_start(out=out[:, cols], in_=res[j][:])

@@ -104,16 +104,16 @@ def tile_attend_gpdirect_twoside_kernel(
             return bank
 
         offsets = sb.tile([P, SLOTS // 16], U16, name="offsets")
-        ks_pool = sb.tile([P, POOL], U8, name="ks_pool", tag="value_words")
+        ks_pool = sb.tile([P, POOL], U8, name="ks_pool")
         vs_pool = sb.tile([P, POOL], U8, name="vs_pool", tag="value_scales")
-        q_raw = sb.tile([P, PACK, ROWS], F32, name="q_raw", tag="staging")
-        v = col("v")
+        q_raw = sb.tile([P, PACK, ROWS], F32, name="q_raw", tag="value_words")
+        v = sb.tile([P, 1], F32, name="v", tag="staging")
         one = sb.tile([P, 1], F32, name="one", tag="key_words", align_bytes=64)
         factors = sb.tile([P, 2], F32, name="factors")
         hv = factors[:, 1:2]
 
-        nc.vector.memset(one[:], 1.0)
         nc.vector.memset(ks_pool[:].bitcast(I32), 0)
+        nc.vector.memset(one[:], 1.0)
         nc.vector.tensor_scalar(factors[:, 0:1], one[:], H, None, ALU.mult)
         nc.vector.memset(vs_pool[:].bitcast(I32), 0)
 
@@ -126,17 +126,16 @@ def tile_attend_gpdirect_twoside_kernel(
         load_scales(vs_pool, vals_scales)
 
         q_bf = interleave("q_bf", q_raw)
+        nc.scalar.activation(hv, v[:], ACT.Identity, scale=H)
+        neg_hv = fma("neg_hv", v[:], -H)
+        neg_v = fma("neg_v", v[:], -1.0)
         g_raw = sb.tile([P, PACK, ROWS], F32, name="g_raw", tag="staging")
         load_rows(g_raw, gout)
-        ks = gather_plane("ks", ks_pool, "key_plane")
         vw_pool = sb.tile([P, POOL], U32, name="vw_pool", tag="value_words")
         load_words(vw_pool, vals_words)
         g_bf = interleave("g_bf", g_raw)
 
-        nc.scalar.activation(hv, v[:], ACT.Identity, scale=H)
-        neg_hv = fma("neg_hv", v[:], -H)
-        neg_v = fma("neg_v", v[:], -1.0)
-
+        ks = gather_plane("ks", ks_pool, "key_plane")
         q_mx = quantise("q", q_bf)
         a = product("a", q_mx, kw_pool, ks, ("q_bf", "a1"))
         vs = gather_plane("vs", vs_pool, "key_words")
@@ -168,7 +167,7 @@ def tile_attend_gpdirect_twoside_kernel(
         nc.scalar.activation(r2[:], p2[:], ACT.Identity, scale=i2)
         sc2 = fma("sc2", k[:], -H)
         sc1 = fma("sc1", k[:], neg_hv[:])
-        kv = fma("kv", k[:], v[:])
+        neg_kv = fma("neg_kv", k[:], neg_v[:])
         nc.scalar.activation(r1[:], p1[:], ACT.Identity, scale=i1)
 
         x1, m1 = wide("x1"), col("m1")
@@ -186,7 +185,6 @@ def tile_attend_gpdirect_twoside_kernel(
         nc.scalar.activation(scratch[0][:], c[:], ACT.Identity, bias=b2[:], scale=sc2[:], accum_out=f2[:])
         dm = fma("dm", m1[:], neg_v[:], m2[:])
         nc.scalar.activation(scratch[1][:], c[:], ACT.Identity, bias=b1[:], scale=sc1[:], accum_out=f1[:])
-        t = fma("t", f2[:], dm[:])
         nc.scalar.activation(scratch[2][:], c[:], ACT.Square, bias=m1[:], scale=-H, accum_out=spread[:])
 
         y = sb.tile([P, 2], F32, name="y")
@@ -199,11 +197,12 @@ def tile_attend_gpdirect_twoside_kernel(
         nc.scalar.activation(sq2[:], u2[:], ACT.Square, bias=y2, scale=-2.0, accum_out=total2[:])
         nc.scalar.activation(sq1[:], u1[:], ACT.Square, bias=y1, scale=-2.0, accum_out=total1[:])
 
-        cross = col("cross")
-        nc.vector.tensor_scalar(cross[:], spread[:], kv[:], t[:], ALU.mult, ALU.add)
+        t, neg_cross = col("t"), col("neg_cross")
+        nc.vector.tensor_tensor(t[:], f2[:], dm[:], ALU.mult)
         yy, rest = sb.tile([P, 2], F32, name="yy"), sb.tile([P, 2], F32, name="rest")
         nc.vector.tensor_tensor(yy[:], y[:], y[:], ALU.mult)
-        nc.vector.tensor_scalar(rest[:], yy[:], -SLOTS / 4.0, cross[:], ALU.mult, ALU.add)
+        nc.vector.tensor_scalar(neg_cross[:], spread[:], neg_kv[:], t[:], ALU.mult, ALU.subtract)
+        nc.vector.tensor_scalar(rest[:], yy[:], -SLOTS / 4.0, neg_cross[:], ALU.mult, ALU.subtract)
         kc1 = fma("kc1", rest[:, 0:1], 4.0, total1[:])
         kc2 = fma("kc2", rest[:, 1:2], 4.0, total2[:])
 

@@ -48,10 +48,10 @@ def tile_attend_gpdirect_twoside_kernel(
                 nc.scalar.activation(t[:], x, ACT.Identity, bias=bias, scale=scale)
             return t
 
-        def load_scales(tile, scales):
+        def load_scales(tile, scales, first, queues):
             for quad in range(4):
-                nc.sync.dma_start(
-                    out=tile[32 * quad : 32 * quad + 4, :].bitcast(I32),
+                queues[quad % len(queues)].dma_start(
+                    out=tile[32 * quad + first : 32 * quad + first + 4, :].bitcast(I32),
                     in_=scales[0, 4 * quad : 4 * quad + 4, :].bitcast(I32),
                 )
 
@@ -69,9 +69,9 @@ def tile_attend_gpdirect_twoside_kernel(
             nc.scalar.copy(out=grouped[:], in_=raw[:].rearrange("p j w -> p w j"))
             return grouped
 
-        def quantise(name, grouped):
-            codes = sb.tile([P, ROWS], U32, name=name + "_codes", align_bytes=64)
-            plane = sb.tile([P, ROWS], U8, name=name + "_plane", align_bytes=64)
+        def quantise(name, grouped, tag):
+            codes = sb.tile([P, ROWS], U32, name=name + "_codes", tag=tag, align_bytes=64)
+            plane = sb.tile([P, ROWS], U8, name=name + "_plane", tag=name + "_plane", align_bytes=64)
             nc.vector.quantize_mx(
                 out=codes[:].bitcast(FP8X4),
                 scales=plane[:],
@@ -86,18 +86,24 @@ def tile_attend_gpdirect_twoside_kernel(
             nc.vector.tensor_copy(out=picked[:], in_=window[:].indirect(offsets[:]))
             return picked
 
-        def product(name, left, window, plane, tags):
-            bank = psum.tile([P, SLOTS], F32, name=name)
-            for j, cols in enumerate(halves):
-                words = sb.tile([P, HALF], U32, name=f"{name}_words{j}", tag=tags[j], align_bytes=64)
+        def gather_words(name, window, tags):
+            parts = []
+            for j in range(2):
+                words = sb.tile([P, HALF], U32, name=f"{name}{j}", tag=tags[j], align_bytes=64)
                 entries = offsets[:, j * HALF // 16 : (j + 1) * HALF // 16]
                 nc.vector.tensor_copy(out=words[:], in_=window[:].indirect(entries))
+                parts.append(words)
+            return parts
+
+        def product(name, left, parts, plane, first):
+            bank = psum.tile([P, SLOTS], F32, name=name)
+            for words, cols in zip(parts, halves):
                 nc.tensor.matmul_mx(
                     out=bank[:, cols],
                     lhsT=left[0][:].bitcast(FP8X4),
                     lhsT_scale=left[1][:],
                     rhs=words[:].bitcast(FP8X4),
-                    rhs_scale=plane[:, cols],
+                    rhs_scale=plane[first:, cols],
                     start=True,
                     stop=True,
                 )
@@ -106,68 +112,70 @@ def tile_attend_gpdirect_twoside_kernel(
         offsets = sb.tile([P, SLOTS // 16], U16, name="offsets")
         ks_pool = sb.tile([P, POOL], U8, name="ks_pool")
         vs_pool = sb.tile([P, POOL], U8, name="vs_pool", tag="value_scales")
-        q_raw = sb.tile([P, PACK, ROWS], F32, name="q_raw", tag="value_words")
+        kw_pool = sb.tile([P, POOL], U32, name="kw_pool")
         v = sb.tile([P, 1], F32, name="v", tag="staging")
-        one = sb.tile([P, 1], F32, name="one", tag="key_words", align_bytes=64)
-        factors = sb.tile([P, 2], F32, name="factors")
-        hv = factors[:, 1:2]
+        one = sb.tile([P, 1], F32, name="one", tag="query_rows", align_bytes=64)
+        h = sb.tile([P, 1], F32, name="h", tag="value_words")
 
         nc.vector.memset(ks_pool[:].bitcast(I32), 0)
         nc.vector.memset(one[:], 1.0)
-        nc.vector.tensor_scalar(factors[:, 0:1], one[:], H, None, ALU.mult)
+        nc.vector.tensor_scalar(h[:], one[:], H, None, ALU.mult)
         nc.vector.memset(vs_pool[:].bitcast(I32), 0)
 
         nc.sync.dma_start(offsets[:], offs)
         nc.sync.dma_start(out=v[:], in_=averse)
-        load_rows(q_raw, query)
-        load_scales(ks_pool, keys_scales)
-        kw_pool = sb.tile([P, POOL], U32, name="kw_pool", tag="key_words", align_bytes=64)
         load_words(kw_pool, keys_words)
-        load_scales(vs_pool, vals_scales)
+        load_scales(ks_pool, keys_scales, 0, (nc.sync,))
+        q_raw = sb.tile([P, PACK, ROWS], F32, name="q_raw", tag="query_rows", align_bytes=64)
+        load_rows(q_raw, query)
+        load_scales(vs_pool, vals_scales, 4, (nc.sync,))
 
-        q_bf = interleave("q_bf", q_raw)
-        nc.scalar.activation(hv, v[:], ACT.Identity, scale=H)
-        neg_hv = fma("neg_hv", v[:], -H)
+        kept_v = fma("kept_v", v[:], 1.0)
         neg_v = fma("neg_v", v[:], -1.0)
+        hv = fma("hv", v[:], h[:])
         g_raw = sb.tile([P, PACK, ROWS], F32, name="g_raw", tag="staging")
         load_rows(g_raw, gout)
         vw_pool = sb.tile([P, POOL], U32, name="vw_pool", tag="value_words")
         load_words(vw_pool, vals_words)
+        q_bf = interleave("q_bf", q_raw)
         g_bf = interleave("g_bf", g_raw)
 
+        kw = gather_words("kw", kw_pool, ("kw0", "kw1"))
         ks = gather_plane("ks", ks_pool, "key_plane")
-        q_mx = quantise("q", q_bf)
-        a = product("a", q_mx, kw_pool, ks, ("q_bf", "a1"))
-        vs = gather_plane("vs", vs_pool, "key_words")
+        q_mx = quantise("q", q_bf, "q_codes")
+        a = product("a", q_mx, kw, ks, 0)
+        vs = gather_plane("vs", vs_pool, "query_rows")
 
         base_sb = sb.tile([P, SLOTS], F32, name="base_sb", tag="key_plane", align_bytes=64)
         nc.sync.dma_start(out=base_sb[:], in_=base)
 
-        neg_max = sb.tile([P, 1], F32, name="neg_max", tag="value_scales")
-        low = col("low")
-        nc.vector.tensor_reduce(out=neg_max[:], in_=a[:], axis=AX.X, op=ALU.max, negate=True)
-        nc.vector.tensor_reduce(out=low[:], in_=a[:], axis=AX.X, op=ALU.min)
-        g_mx = quantise("g", g_bf)
+        ends = sb.tile([P, 2], F32, name="ends", tag="value_scales")
+        neg_max, low = ends[:, 0:1], ends[:, 1:2]
+        nc.vector.tensor_reduce(out=neg_max, in_=a[:], axis=AX.X, op=ALU.max, negate=True)
+        nc.vector.tensor_reduce(out=low, in_=a[:], axis=AX.X, op=ALU.min)
+        g_mx = quantise("g", g_bf, "kw1")
         p1 = sb.tile([P, SLOTS], F32, name="p1", tag="staging")
         p2 = wide("p2")
         sums = sb.tile([P, 2], F32, name="sums")
-        nc.scalar.activation(p1[:], a[:], ACT.Exp, bias=neg_max[:], scale=1.0, accum_out=sums[:, 0:1])
-        nc.scalar.activation(p2[:], a[:], ACT.Exp, bias=low[:], scale=-1.0, accum_out=sums[:, 1:2])
+        nc.scalar.activation(p1[:], a[:], ACT.Exp, bias=neg_max, scale=1.0, accum_out=sums[:, 0:1])
+        nc.scalar.activation(p2[:], a[:], ACT.Exp, bias=low, scale=-1.0, accum_out=sums[:, 1:2])
         k0 = col("k0")
-        nc.scalar.activation(k0[:], low[:], ACT.Exp, bias=neg_max[:], scale=1.0)
-        c = product("c", g_mx, vw_pool, vs, ("g_bf", "c1"))
+        nc.scalar.activation(k0[:], low, ACT.Exp, bias=neg_max, scale=1.0)
+        vw = gather_words("vw", vw_pool, ("q_codes", "q_plane"))
+        c = product("c", g_mx, vw, vs, 4)
 
         inv = sb.tile([P, 2], F32, name="inv", tag="value_words")
         nc.vector.reciprocal(out=inv[:], in_=sums[:])
         i1, i2 = inv[:, 0:1], inv[:, 1:2]
         hi, k = sb.tile([P, 2], F32, name="hi"), col("k")
-        nc.vector.tensor_tensor(hi[:], inv[:], factors[:], ALU.mult)
+        nc.vector.tensor_scalar(hi[:, 0:1], i1, H, None, ALU.mult)
+        nc.vector.tensor_scalar(hi[:, 1:2], i2, hv[:], None, ALU.mult)
         nc.vector.tensor_scalar(k[:], k0[:], i1, i2, ALU.mult, ALU.mult)
         r1, r2 = wide("r1"), wide("r2")
         nc.scalar.activation(r2[:], p2[:], ACT.Identity, scale=i2)
         sc2 = fma("sc2", k[:], -H)
-        sc1 = fma("sc1", k[:], neg_hv[:])
-        neg_kv = fma("neg_kv", k[:], neg_v[:])
+        nk = fma("nk", k[:], float(SLOTS))
+        kv = fma("kv", k[:], kept_v[:])
         nc.scalar.activation(r1[:], p1[:], ACT.Identity, scale=i1)
 
         x1, m1 = wide("x1"), col("m1")
@@ -179,41 +187,39 @@ def tile_attend_gpdirect_twoside_kernel(
         nc.vector.scalar_tensor_tensor(u1[:], r1[:], m1[:], x1[:], ALU.mult, ALU.subtract)
 
         b2 = fma("b2", m1[:], k[:])
-        b1 = fma("b1", m2[:], k[:])
-        scratch = [wide(f"scratch{j}") for j in range(3)]
-        f1, f2, spread = col("f1"), col("f2"), col("spread")
-        nc.scalar.activation(scratch[0][:], c[:], ACT.Identity, bias=b2[:], scale=sc2[:], accum_out=f2[:])
         dm = fma("dm", m1[:], neg_v[:], m2[:])
-        nc.scalar.activation(scratch[1][:], c[:], ACT.Identity, bias=b1[:], scale=sc1[:], accum_out=f1[:])
-        nc.scalar.activation(scratch[2][:], c[:], ACT.Square, bias=m1[:], scale=-H, accum_out=spread[:])
+        scratch = [wide(f"scratch{j}") for j in range(2)]
+        f2, spread = col("f2"), col("spread")
+        nc.scalar.activation(scratch[0][:], c[:], ACT.Identity, bias=b2[:], scale=sc2[:], accum_out=f2[:])
+        e = fma("e", dm[:], nk[:])
+        nc.scalar.activation(scratch[1][:], c[:], ACT.Square, bias=m1[:], scale=-H, accum_out=spread[:])
+        f1 = fma("f1", f2[:], kept_v[:], e[:])
+        t = fma("t", f2[:], dm[:])
+        cross = fma("cross", spread[:], kv[:], t[:])
 
-        y = sb.tile([P, 2], F32, name="y")
-        y1, y2 = y[:, 0:1], y[:, 1:2]
+        y1, y2, yy1, yy2 = col("y1"), col("y2"), col("yy1"), col("yy2")
         w1, w2 = wide("w1"), wide("w2")
-        nc.vector.scalar_tensor_tensor(w2[:], u2[:], f2[:], r2[:], ALU.add, ALU.mult, accum_out=y2)
-        nc.vector.scalar_tensor_tensor(w1[:], u1[:], f1[:], r1[:], ALU.add, ALU.mult, accum_out=y1)
+        nc.vector.scalar_tensor_tensor(w2[:], u2[:], f2[:], r2[:], ALU.add, ALU.mult, accum_out=y2[:])
+        nc.vector.scalar_tensor_tensor(w1[:], u1[:], f1[:], r1[:], ALU.add, ALU.mult, accum_out=y1[:])
+        nc.vector.tensor_tensor(yy2[:], y2[:], y2[:], ALU.mult)
+        nc.vector.tensor_tensor(yy1[:], y1[:], y1[:], ALU.mult)
 
         sq1, sq2, total1, total2 = wide("sq1"), wide("sq2"), col("total1"), col("total2")
-        nc.scalar.activation(sq2[:], u2[:], ACT.Square, bias=y2, scale=-2.0, accum_out=total2[:])
-        nc.scalar.activation(sq1[:], u1[:], ACT.Square, bias=y1, scale=-2.0, accum_out=total1[:])
-
-        t, neg_cross = col("t"), col("neg_cross")
-        nc.vector.tensor_tensor(t[:], f2[:], dm[:], ALU.mult)
-        yy, rest = sb.tile([P, 2], F32, name="yy"), sb.tile([P, 2], F32, name="rest")
-        nc.vector.tensor_tensor(yy[:], y[:], y[:], ALU.mult)
-        nc.vector.tensor_scalar(neg_cross[:], spread[:], neg_kv[:], t[:], ALU.mult, ALU.subtract)
-        nc.vector.tensor_scalar(rest[:], yy[:], -SLOTS / 4.0, neg_cross[:], ALU.mult, ALU.subtract)
-        kc1 = fma("kc1", rest[:, 0:1], 4.0, total1[:])
-        kc2 = fma("kc2", rest[:, 1:2], 4.0, total2[:])
+        nc.scalar.activation(sq2[:], u2[:], ACT.Square, bias=y2[:], scale=-2.0, accum_out=total2[:])
+        nc.scalar.activation(sq1[:], u1[:], ACT.Square, bias=y1[:], scale=-2.0, accum_out=total1[:])
+        rest1 = fma("rest1", yy1[:], -SLOTS / 4.0, cross[:])
+        rest2 = fma("rest2", yy2[:], -SLOTS / 4.0, cross[:])
+        kc1 = fma("kc1", rest1[:], 4.0, total1[:])
+        kc2 = fma("kc2", rest2[:], 4.0, total2[:])
 
         ta = [sb.tile([P, HALF], F32, name=f"ta{j}") for j in range(2)]
         tb = [sb.tile([P, HALF], F32, name=f"tb{j}") for j in range(2)]
         td = [sb.tile([P, HALF], F32, name=f"td{j}") for j in range(2)]
         res = [sb.tile([P, HALF], F32, name=f"res{j}") for j in range(2)]
         for j, cols in enumerate(halves):
-            nc.vector.scalar_tensor_tensor(ta[j][:], sq2[:, cols], yy[:, 1:2], base_sb[:, cols], ALU.subtract, ALU.subtract)
+            nc.vector.scalar_tensor_tensor(ta[j][:], sq2[:, cols], yy2[:], base_sb[:, cols], ALU.subtract, ALU.subtract)
         for j, cols in enumerate(halves):
-            nc.vector.scalar_tensor_tensor(tb[j][:], sq1[:, cols], yy[:, 0:1], ta[j][:], ALU.subtract, ALU.subtract)
+            nc.vector.scalar_tensor_tensor(tb[j][:], sq1[:, cols], yy1[:], ta[j][:], ALU.subtract, ALU.subtract)
         for j, cols in enumerate(halves):
             nc.vector.scalar_tensor_tensor(td[j][:], r1[:, cols], kc1[:], tb[j][:], ALU.mult, ALU.subtract)
         for j, cols in enumerate(halves):

import math
from contextlib import ExitStack

import concourse.mybir as mybir

F32 = mybir.dt.float32
BF16 = mybir.dt.bfloat16
I32 = mybir.dt.int32
U32 = mybir.dt.uint32
U16 = mybir.dt.uint16
U8 = mybir.dt.uint8
FP8X4 = mybir.dt.float8_e4m3fn_x4
ALU = mybir.AluOpType
ACT = mybir.ActivationFunctionType
AX = mybir.AxisListType

P = 128
PACK = 4
POOL = 2048
SLOTS = 512
ROWS = 128
FEATS = 512
HALF = SLOTS // 2
H = math.sqrt(512.0 * 2.0 * 512.0) / 2.0

FLOPS = 2 * 2 * FEATS * ROWS * SLOTS


def tile_attend_gpdirect_twoside_kernel(
    tc, query, keys_words, keys_scales, averse, gout, vals_words, vals_scales, base, offs, out
):
    nc = tc.nc
    with ExitStack() as ctx:
        sb = ctx.enter_context(tc.tile_pool(name="sb", bufs=1))
        psum = ctx.enter_context(tc.psum_pool(name="psum", bufs=1))

        def wide(name):
            return sb.tile([P, SLOTS], F32, name=name)

        def col(name):
            return sb.tile([P, 1], F32, name=name)

        def fma(name, x, scale, bias=None):
            t = col(name)
            if bias is None:
                nc.scalar.activation(t[:], x, ACT.Identity, scale=scale)
            else:
                nc.scalar.activation(t[:], x, ACT.Identity, bias=bias, scale=scale)
            return t

        def load_scales(tile, scales, first, queues):
            for quad in range(4):
                queues[quad % len(queues)].dma_start(
                    out=tile[32 * quad + first : 32 * quad + first + 4, :].bitcast(I32),
                    in_=scales[0, 4 * quad : 4 * quad + 4, :].bitcast(I32),
                )

        def load_words(tile, words):
            nc.sync.dma_start(
                out=tile[:].bitcast(I32),
                in_=words[0].rearrange("p n t -> p (n t)").bitcast(I32),
            )

        def load_rows(tile, rows):
            nc.sync.dma_start(out=tile[:], in_=rows.rearrange("(p j) w -> p j w", j=PACK))

        def interleave(name, raw):
            grouped = sb.tile([P, ROWS, PACK], BF16, name=name, tag=name, align_bytes=64)
            nc.scalar.copy(out=grouped[:], in_=raw[:].rearrange("p j w -> p w j"))
            return grouped

        def quantise(name, grouped, tag):
            codes = sb.tile([P, ROWS], U32, name=name + "_codes", tag=tag, align_bytes=64)
            plane = sb.tile([P, ROWS], U8, name=name + "_plane", tag=name + "_plane", align_bytes=64)
            nc.vector.quantize_mx(
                out=codes[:].bitcast(FP8X4),
                scales=plane[:],
                in_=grouped[:].rearrange("p w j -> p (w j)"),
            )
            return codes, plane

        halves = [slice(0, HALF), slice(HALF, SLOTS)]

        def gather_plane(name, window, tag):
            picked = sb.tile([P, SLOTS], U8, name=name, tag=tag, align_bytes=64)
            nc.vector.tensor_copy(out=picked[:], in_=window[:].indirect(offsets[:]))
            return picked

        def gather_words(name, window, tags):
            parts = []
            for j in range(2):
                words = sb.tile([P, HALF], U32, name=f"{name}{j}", tag=tags[j], align_bytes=64)
                entries = offsets[:, j * HALF // 16 : (j + 1) * HALF // 16]
                nc.vector.tensor_copy(out=words[:], in_=window[:].indirect(entries))
                parts.append(words)
            return parts

        def product(name, left, parts, plane, first):
            bank = psum.tile([P, SLOTS], F32, name=name)
            for words, cols in zip(parts, halves):
                nc.tensor.matmul_mx(
                    out=bank[:, cols],
                    lhsT=left[0][:].bitcast(FP8X4),
                    lhsT_scale=left[1][:],
                    rhs=words[:].bitcast(FP8X4),
                    rhs_scale=plane[first:, cols],
                    start=True,
                    stop=True,
                )
            return bank

        offsets = sb.tile([P, SLOTS // 16], U16, name="offsets")
        ks_pool = sb.tile([P, POOL], U8, name="ks_pool")
        vs_pool = sb.tile([P, POOL], U8, name="vs_pool", tag="value_scales")
        kw_pool = sb.tile([P, POOL], U32, name="kw_pool")
        v = sb.tile([P, 1], F32, name="v", tag="staging")
        one = sb.tile([P, 1], F32, name="one", tag="query_rows", align_bytes=64)
        h = sb.tile([P, 1], F32, name="h", tag="value_words")

        nc.vector.memset(ks_pool[:].bitcast(I32), 0)
        nc.vector.memset(one[:], 1.0)
        nc.vector.tensor_scalar(h[:], one[:], H, None, ALU.mult)
        nc.vector.memset(vs_pool[:].bitcast(I32), 0)

        nc.sync.dma_start(offsets[:], offs)
        nc.sync.dma_start(out=v[:], in_=averse)
        load_words(kw_pool, keys_words)
        load_scales(ks_pool, keys_scales, 0, (nc.sync,))
        q_raw = sb.tile([P, PACK, ROWS], F32, name="q_raw", tag="query_rows", align_bytes=64)
        load_rows(q_raw, query)
        load_scales(vs_pool, vals_scales, 4, (nc.sync,))

        kept_v = fma("kept_v", v[:], 1.0)
        neg_v = fma("neg_v", v[:], -1.0)
        hv = fma("hv", v[:], h[:])
        g_raw = sb.tile([P, PACK, ROWS], F32, name="g_raw", tag="staging")
        load_rows(g_raw, gout)
        vw_pool = sb.tile([P, POOL], U32, name="vw_pool", tag="value_words")
        load_words(vw_pool, vals_words)
        q_bf = interleave("q_bf", q_raw)
        g_bf = interleave("g_bf", g_raw)

        kw = gather_words("kw", kw_pool, ("kw0", "kw1"))
        ks = gather_plane("ks", ks_pool, "key_plane")
        q_mx = quantise("q", q_bf, "q_codes")
        a = product("a", q_mx, kw, ks, 0)
        vs = gather_plane("vs", vs_pool, "query_rows")

        base_sb = sb.tile([P, SLOTS], F32, name="base_sb", tag="key_plane", align_bytes=64)
        nc.sync.dma_start(out=base_sb[:], in_=base)

        ends = sb.tile([P, 2], F32, name="ends", tag="value_scales")
        neg_max, low = ends[:, 0:1], ends[:, 1:2]
        nc.vector.tensor_reduce(out=neg_max, in_=a[:], axis=AX.X, op=ALU.max, negate=True)
        nc.vector.tensor_reduce(out=low, in_=a[:], axis=AX.X, op=ALU.min)
        g_mx = quantise("g", g_bf, "kw1")
        p1 = sb.tile([P, SLOTS], F32, name="p1", tag="staging")
        p2 = wide("p2")
        sums = sb.tile([P, 2], F32, name="sums")
        nc.scalar.activation(p1[:], a[:], ACT.Exp, bias=neg_max, scale=1.0, accum_out=sums[:, 0:1])
        nc.scalar.activation(p2[:], a[:], ACT.Exp, bias=low, scale=-1.0, accum_out=sums[:, 1:2])
        k0 = col("k0")
        nc.scalar.activation(k0[:], low, ACT.Exp, bias=neg_max, scale=1.0)
        vw = gather_words("vw", vw_pool, ("q_codes", "q_plane"))
        c = product("c", g_mx, vw, vs, 4)

        inv = sb.tile([P, 2], F32, name="inv", tag="value_words")
        nc.vector.reciprocal(out=inv[:], in_=sums[:])
        i1, i2 = inv[:, 0:1], inv[:, 1:2]
        hi, k = sb.tile([P, 2], F32, name="hi"), col("k")
        nc.vector.tensor_scalar(hi[:, 0:1], i1, H, None, ALU.mult)
        nc.vector.tensor_scalar(hi[:, 1:2], i2, hv[:], None, ALU.mult)
        nc.vector.tensor_scalar(k[:], k0[:], i1, i2, ALU.mult, ALU.mult)
        r1, r2 = wide("r1"), wide("r2")
        nc.scalar.activation(r2[:], p2[:], ACT.Identity, scale=i2)
        sc2 = fma("sc2", k[:], -H)
        nk = fma("nk", k[:], float(SLOTS))
        kv = fma("kv", k[:], kept_v[:])
        nc.scalar.activation(r1[:], p1[:], ACT.Identity, scale=i1)

        x1, m1 = wide("x1"), col("m1")
        nc.vector.scalar_tensor_tensor(x1[:], c[:], hi[:, 0:1], p1[:], ALU.mult, ALU.mult, accum_out=m1[:])
        x2, m2 = wide("x2"), col("m2")
        nc.vector.scalar_tensor_tensor(x2[:], c[:], hi[:, 1:2], p2[:], ALU.mult, ALU.mult, accum_out=m2[:])
        u1, u2 = wide("u1"), wide("u2")
        nc.vector.scalar_tensor_tensor(u2[:], r2[:], m2[:], x2[:], ALU.mult, ALU.subtract)
        nc.vector.scalar_tensor_tensor(u1[:], r1[:], m1[:], x1[:], ALU.mult, ALU.subtract)

        b2 = fma("b2", m1[:], k[:])
        dm = fma("dm", m1[:], neg_v[:], m2[:])
        scratch = [wide(f"scratch{j}") for j in range(2)]
        f2, spread = col("f2"), col("spread")
        nc.scalar.activation(scratch[0][:], c[:], ACT.Identity, bias=b2[:], scale=sc2[:], accum_out=f2[:])
        e = fma("e", dm[:], nk[:])
        nc.scalar.activation(scratch[1][:], c[:], ACT.Square, bias=m1[:], scale=-H, accum_out=spread[:])
        f1 = fma("f1", f2[:], kept_v[:], e[:])
        t = fma("t", f2[:], dm[:])
        cross = fma("cross", spread[:], kv[:], t[:])

        y1, y2, yy1, yy2 = col("y1"), col("y2"), col("yy1"), col("yy2")
        w1, w2 = wide("w1"), wide("w2")
        nc.vector.scalar_tensor_tensor(w2[:], u2[:], f2[:], r2[:], ALU.add, ALU.mult, accum_out=y2[:])
        nc.vector.scalar_tensor_tensor(w1[:], u1[:], f1[:], r1[:], ALU.add, ALU.mult, accum_out=y1[:])
        nc.vector.tensor_tensor(yy2[:], y2[:], y2[:], ALU.mult)
        nc.vector.tensor_tensor(yy1[:], y1[:], y1[:], ALU.mult)

        sq1, sq2, total1, total2 = wide("sq1"), wide("sq2"), col("total1"), col("total2")
        nc.scalar.activation(sq2[:], u2[:], ACT.Square, bias=y2[:], scale=-2.0, accum_out=total2[:])
        nc.scalar.activation(sq1[:], u1[:], ACT.Square, bias=y1[:], scale=-2.0, accum_out=total1[:])
        rest1 = fma("rest1", yy1[:], -SLOTS / 4.0, cross[:])
        rest2 = fma("rest2", yy2[:], -SLOTS / 4.0, cross[:])
        kc1 = fma("kc1", rest1[:], 4.0, total1[:])
        kc2 = fma("kc2", rest2[:], 4.0, total2[:])

        ta = [sb.tile([P, HALF], F32, name=f"ta{j}") for j in range(2)]
        tb = [sb.tile([P, HALF], F32, name=f"tb{j}") for j in range(2)]
        td = [sb.tile([P, HALF], F32, name=f"td{j}") for j in range(2)]
        res = [sb.tile([P, HALF], F32, name=f"res{j}") for j in range(2)]
        for j, cols in enumerate(halves):
            nc.vector.scalar_tensor_tensor(ta[j][:], sq2[:, cols], yy2[:], base_sb[:, cols], ALU.subtract, ALU.subtract)
        for j, cols in enumerate(halves):
            nc.vector.scalar_tensor_tensor(tb[j][:], sq1[:, cols], yy1[:], ta[j][:], ALU.subtract, ALU.subtract)
        for j, cols in enumerate(halves):
            nc.vector.scalar_tensor_tensor(td[j][:], r1[:, cols], kc1[:], tb[j][:], ALU.mult, ALU.subtract)
        for j, cols in enumerate(halves):
            nc.vector.scalar_tensor_tensor(res[j][:], r2[:, cols], kc2[:], td[j][:], ALU.mult, ALU.subtract)
            nc.sync.dma_start(out=out[:, cols], in_=res[j][:])
